import numpy as np
import ml_dtypes


def mxq(x, axis, fmt="e4m3"):
    dtype, down = {"e4m3": (ml_dtypes.float8_e4m3fn, 7), "e5m2": (ml_dtypes.float8_e5m2, 14)}[fmt]
    v = np.moveaxis(np.asarray(x, np.float32).astype(ml_dtypes.bfloat16).astype(np.float64), axis, -1)
    blocks = v.reshape(v.shape[:-1] + (-1, 32))
    amax = np.abs(blocks).max(-1, keepdims=True)
    byte = np.maximum(np.where(amax > 0, np.frexp(amax)[1] - 1 + 127, 0) - down, 1)
    scale = np.exp2(byte - 127.0)
    codes = (blocks / scale).astype(np.float32).astype(dtype).astype(np.float64)
    return np.moveaxis((codes * scale).reshape(v.shape), -1, axis)


WIDE = False


def mx_kscale(k):
    if not WIDE:
        return np.ones(k)
    levels = np.array([10, -10, 5, -5, 0])
    if k % 512:
        return np.exp2(np.random.permutation(np.resize(levels, k // 32))).repeat(32)
    a = np.empty((k // 512, 16))
    for p in range(k // 512):
        a[p, :8] = np.random.permutation(np.resize(levels, 8))
        for g in range(8):
            far = levels[np.abs(levels - a[p, g]) >= 10]
            a[p, g + 8] = far[np.random.randint(len(far))]
    return np.exp2(a.ravel()).repeat(32)


def f64(x):
    return np.asarray(x).astype(np.float64)


def striped(idx):
    return np.tile(idx.reshape(-1, 16).T, (8, 1)).astype(np.uint16)


def unstriped(offs):
    return offs[:16].T.reshape(-1).astype(np.int64)


E2M1 = np.array([0.0, 0.5, 1.0, 1.5, 2.0, 3.0, 4.0, 6.0, -0.0, -0.5, -1.0, -1.5, -2.0, -3.0, -4.0, -6.0])


def pack_weight(w, fmt):
    k, n = w.shape
    w = f64(np.asarray(w, np.float32).astype(ml_dtypes.bfloat16)).reshape(k // 32, 32, n)
    amax = np.abs(w).max(1)
    if fmt == "e4m3":
        byte = np.frexp(amax)[1] - 1 + 127 - 7
    else:
        mant, ex = np.frexp(amax / 6.0)
        byte = np.where(mant > 0.5, ex, ex - 1) + 127
    byte = np.clip(np.where(amax > 0, byte, 1), 1, 254)
    scaled = (w * np.exp2(127.0 - byte)[:, None, :]).reshape(k, n).astype(np.float32)
    by_word = np.ascontiguousarray(scaled.reshape(k // 512, 128, 4, n).transpose(0, 1, 3, 2))
    if fmt == "e4m3":
        words = by_word.astype(ml_dtypes.float8_e4m3fn).view(np.uint8)
    else:
        c = by_word.astype(ml_dtypes.float4_e2m1fn).view(np.uint8) & 0xF
        words = (c[..., 0::2] | (c[..., 1::2] << 4)).reshape(k // 512, 128, 2 * n)
    return np.ascontiguousarray(words), np.ascontiguousarray(byte.astype(np.uint8).reshape(k // 512, 16, n))


def unpack_weight(words, scales, fmt):
    g, _, n = scales.shape
    words = np.ascontiguousarray(words).reshape(g, 128, n, -1)
    if fmt == "e4m3":
        vals = words.view(ml_dtypes.float8_e4m3fn).astype(np.float64)
    else:
        nib = np.empty((g, 128, n, 4), np.uint8)
        nib[..., 0::2] = words & 0xF
        nib[..., 1::2] = words >> 4
        vals = E2M1[nib]
    vals = vals * np.repeat(np.exp2(scales.astype(np.float64) - 127.0), 8, axis=1)[..., None]
    return vals.transpose(0, 1, 3, 2).reshape(g * 512, n)


def gelu(v):
    return 0.5 * v * (1.0 + np.tanh(np.sqrt(2.0 / np.pi) * (v + 0.044715 * v**3)))


def bf(x):
    return np.asarray(x, np.float32).astype(ml_dtypes.bfloat16)


def planes(Y):
    n, m = Y.shape
    b = f64(bf(Y)).reshape(n // 32, 32, m)
    amax = np.abs(b).max(1)
    byte = np.clip(np.where(amax > 0, np.frexp(amax)[1] - 1 + 127 - 7, 1), 1, 254)
    codes = (b * np.exp2(127.0 - byte)[:, None, :]).reshape(n, m).astype(np.float32).astype(ml_dtypes.float8_e4m3fn).view(np.uint8)
    words = codes.reshape(n // 512, 128, 4, m).transpose(0, 1, 3, 2)
    return np.ascontiguousarray(words), np.ascontiguousarray(byte.astype(np.uint8).reshape(n // 512, 16, m))


K, T, S, P, H, N = 1536, 2048, 1024, 512, 1024, 512

def setup_inputs():
    n = np.random.standard_normal
    s = mx_kscale(K)[:, None]
    u = mx_kscale(H)[:, None]
    tab_words, tab_scales = pack_weight(n((K, T)) * s, "e4m3")
    w1 = n((K, H)) * (1.3 / np.sqrt(K)) / s
    gain = np.random.uniform(0.6, 1.6, H) * u[:, 0]
    w4_words, w4_scales = pack_weight(n((H, N)) / np.sqrt(H) / u, "e2m1")
    steep = np.random.uniform(1, 3, N)
    share = np.random.uniform(0.1, 0.5, N)
    worth = np.random.uniform(0.8, 2.4, N) * np.sign(n(N))
    level = np.exp(0.8 * n(N))
    return {
        "tab_words": tab_words, "tab_scales": tab_scales,
        "w1": w1.astype(np.float32), "gain": gain.astype(np.float32),
        "w4_words": w4_words, "w4_scales": w4_scales,
        "steep": steep.astype(np.float32), "share": share.astype(np.float32),
        "worth": worth.astype(np.float32), "level": level.astype(np.float32),
        "offs": striped(np.random.permutation(T)[:S]),
        "pos1": striped(np.random.permutation(S)[:P]),
        "pos2": striped(np.random.permutation(S)[:P]),
    }

def reference(tab_words, tab_scales, w1, gain, w4_words, w4_scales, steep, share, worth, level, offs, pos1, pos2):
    v = unpack_weight(tab_words, tab_scales, "e4m3")[:, unstriped(offs)]
    w4 = unpack_weight(w4_words, w4_scales, "e2m1")
    h = np.tanh(mxq(f64(w1), 0, "e4m3").T @ v) * f64(gain)[:, None]
    e = w4.T @ mxq(h, 0, "e4m3")
    top = e.max(axis=1)
    a = 1.0 / (1.0 + np.exp(-f64(steep)[:, None] * (e[:, unstriped(pos1)] - f64(share)[:, None] * top[:, None])))
    c = e[:, unstriped(pos2)]
    y = f64(level)[:, None] * np.maximum(f64(worth)[:, None] * a, c)
    words, scales = planes(y)
    return y, words, scales

@@ -1,0 +1,312 @@
+from contextlib import ExitStack
+
+import concourse.mybir as mybir
+
+K, T, S, M, H, N = 1536, 2048, 1024, 512, 1024, 512
+FLOPS = 2 * K * H * S + 2 * H * N * S
+
+F32 = mybir.dt.float32
+BF16 = mybir.dt.bfloat16
+I32 = mybir.dt.int32
+U32 = mybir.dt.uint32
+U16 = mybir.dt.uint16
+U8 = mybir.dt.uint8
+FP8X4 = mybir.dt.float8_e4m3fn_x4
+FP4X4 = mybir.dt.float4_e2m1fn_x4
+ALU = mybir.AluOpType
+ACT = mybir.ActivationFunctionType
+
+P = 128
+PACK = 4
+PASS = P * PACK
+KP = K // PASS
+HP = H // PASS
+CH = 128
+NCH = S // CH
+HALF = 512
+
+
+def tile_list_prefetch_zone_scores_kernel(
+    tc, tab_words, tab_scales, w1, gain, w4_words, w4_scales, steep, share, worth, level,
+    offs, pos1, pos2, out_0, out_1, out_2,
+):
+    nc = tc.nc
+    with ExitStack() as ctx:
+        keep = ctx.enter_context(tc.tile_pool(name="keep", bufs=1))
+        ring = ctx.enter_context(tc.tile_pool(name="ring", bufs=4))
+        psum = ctx.enter_context(tc.psum_pool(name="psum", bufs=1))
+
+        offs_sb = keep.tile([P, S // 16], U16, name="offs_sb")
+        pos1_sb = keep.tile([P, M // 16], U16, name="pos1_sb")
+        pos2_sb = keep.tile([P, M // 16], U16, name="pos2_sb")
+        tab_w = [keep.tile([P, T], U32, name=f"tab_w{a}", align_bytes=64) for a in range(KP)]
+        tab_s = keep.tile([P, T], U8, name="tab_s", align_bytes=64)
+        w1_raw = {(b, a): keep.tile([P, PACK, PASS], F32, name=f"w1_raw{b}{a}", align_bytes=64)
+                  for b in range(HP) for a in range(KP)}
+        w4_raw = keep.tile([P, HP, 2 * N], U8, name="w4_raw", align_bytes=64)
+        w4_sraw = keep.tile([P, HP, N], U8, name="w4_sraw", align_bytes=64)
+        gain_sb = keep.tile([P, HP, PACK], F32, name="gain_sb")
+        steep_sb = keep.tile([P, PACK], F32, name="steep_sb")
+        share_sb = keep.tile([P, PACK], F32, name="share_sb")
+        worth_sb = keep.tile([P, PACK], F32, name="worth_sb")
+        level_sb = keep.tile([P, PACK], F32, name="level_sb")
+
+        def load_tab(a):
+            nc.sync.dma_start(tab_w[a][:].bitcast(I32),
+                              tab_words[a].rearrange("p t i -> p (t i)").bitcast(I32))
+
+        def load_w1(b, a):
+            rows = w1[a * PASS:(a + 1) * PASS, b * PASS:(b + 1) * PASS]
+            nc.sync.dma_start(w1_raw[b, a][:], rows.rearrange("(p j) c -> p j c", j=PACK))
+
+        nc.vector.memset(tab_s[:].bitcast(I32), 0)
+        nc.vector.memset(w4_sraw[:].bitcast(I32), 0)
+        nc.scalar.dma_start(gain_sb[:], gain.rearrange("(b p t) -> p b t", b=HP, t=PACK))
+        nc.sync.dma_start(offs_sb[:], offs)
+        nc.sync.dma_start(w4_raw[:].bitcast(I32), w4_words.rearrange("b p c -> p b c").bitcast(I32))
+        load_tab(0)
+        load_w1(0, 0)
+        for q in range(4):
+            nc.sync.dma_start(tab_s[32 * q:32 * q + 4 * KP, :].bitcast(I32),
+                              tab_scales[:, 4 * q:4 * q + 4, :].bitcast(I32))
+        load_tab(1)
+        load_w1(0, 1)
+        for q in range(4):
+            nc.sync.dma_start(
+                w4_sraw[32 * q:32 * q + 4, :, :].bitcast(I32),
+                w4_scales[:, 4 * q:4 * q + 4, :].rearrange("b r c -> r b c").bitcast(I32))
+        load_w1(0, 2)
+        load_tab(2)
+        for a in range(KP):
+            load_w1(1, a)
+        for vec_sb, vec in ((steep_sb, steep), (share_sb, share), (worth_sb, worth), (level_sb, level)):
+            nc.sync.dma_start(vec_sb[:], vec.rearrange("(p t) -> p t", t=PACK))
+        nc.sync.dma_start(pos1_sb[:], pos1)
+        nc.sync.dma_start(pos2_sb[:], pos2)
+
+        w4_w = keep.tile([P, HP, PACK, 2 * P], U8, name="w4_w", align_bytes=64)
+        w4_s = keep.tile([P, HP, PACK, P], U8, name="w4_s", align_bytes=64)
+        nc.vector.tensor_copy(out=w4_w[:].rearrange("p b t (m e) -> p b m t e", e=2),
+                              in_=w4_raw[:].rearrange("p b (m t e) -> p b m t e", t=PACK, e=2))
+
+        v_w = [keep.tile([P, S], U32, name=f"v_w{a}", align_bytes=64) for a in range(KP)]
+        v_s = keep.tile([P, S], U8, name="v_s", align_bytes=64)
+
+        def gather_words(a, j0, j1):
+            nc.vector.tensor_copy(out=v_w[a][:, j0:j1],
+                                  in_=tab_w[a][:].indirect(offs_sb[:, j0 // 16:j1 // 16]))
+
+        w1_bf = {}
+        w1_w = {}
+        w1_s = {}
+
+        def round_w1(b, a, shares):
+            w1_bf[b, a] = ring.tile([P, PACK, P, PACK], BF16, name="w1_bf", bufs=3, align_bytes=64)
+            dst = w1_bf[b, a][:].rearrange("p t m j -> p m j t")
+            src = w1_raw[b, a][:].rearrange("p j (m t) -> p m j t", t=PACK)
+            for engine, m0, m1 in shares:
+                if engine == "scalar":
+                    nc.scalar.activation(out=dst[:, m0:m1], in_=src[:, m0:m1], func=ACT.Copy)
+                else:
+                    nc.vector.tensor_copy(out=dst[:, m0:m1], in_=src[:, m0:m1])
+
+        def quantize_w1(b, a):
+            w1_w[b, a] = keep.tile([P, PASS], U32, name=f"w1_w{b}{a}", align_bytes=64)
+            w1_s[b, a] = keep.tile([P, PASS], U8, name=f"w1_s{b}{a}", align_bytes=64)
+            nc.vector.quantize_mx(out=w1_w[b, a][:].bitcast(FP8X4), scales=w1_s[b, a][:],
+                                  in_=w1_bf[b, a][:].rearrange("p t m j -> p (t m j)"))
+
+        acc = {}
+
+        def first_pass(b, a, c):
+            if a == 0:
+                acc[b, c] = psum.tile([P, PACK, CH], F32, name=f"acc{b}{c}", tag=f"bank{c}")
+            cols = slice(c * CH, (c + 1) * CH)
+            for t in range(PACK):
+                rows = slice(t * P, (t + 1) * P)
+                nc.tensor.matmul_mx(
+                    out=acc[b, c][:, t, :],
+                    lhsT=w1_w[b, a][:, rows].bitcast(FP8X4), lhsT_scale=w1_s[b, a][:, rows],
+                    rhs=v_w[a][:, cols].bitcast(FP8X4), rhs_scale=v_s[4 * a:P, cols],
+                    start=(a == 0 and t == 0), stop=(a == KP - 1 and t == PACK - 1))
+
+        tanh_sb = {}
+        h_bf = {}
+        h_w = {}
+        h_s = {}
+
+        def tanh_chunk(b, c):
+            if c % 2 == 0:
+                tanh_sb[b, c // 2] = ring.tile([P, 2, CH, PACK], F32, name="tanh_sb", align_bytes=64)
+            nc.scalar.activation(out=tanh_sb[b, c // 2][:, c % 2],
+                                 in_=acc[b, c][:].rearrange("p t n -> p n t"), func=ACT.Tanh)
+
+        def gain_pair(b, d):
+            h_bf[b, d] = ring.tile([P, 2 * CH, PACK], BF16, name="h_bf", align_bytes=64)
+            nc.vector.tensor_tensor(
+                out=h_bf[b, d][:], in0=tanh_sb[b, d][:].rearrange("p c n t -> p (c n) t"),
+                in1=gain_sb[:, b:b + 1, :].to_broadcast([P, 2 * CH, PACK]), op=ALU.mult)
+
+        def quantize_h(b, d):
+            half = d // 2
+            if d % 2 == 0:
+                h_w[b, half] = keep.tile([P, HALF], U32, name=f"h_w{b}{half}", align_bytes=64)
+                h_s[b, half] = keep.tile([P, HALF], U8, name=f"h_s{b}{half}", align_bytes=64)
+            cols = slice((d % 2) * 2 * CH, (d % 2 + 1) * 2 * CH)
+            nc.vector.quantize_mx(out=h_w[b, half][:, cols].bitcast(FP8X4), scales=h_s[b, half][:, cols],
+                                  in_=h_bf[b, d][:].rearrange("p n t -> p (n t)"))
+
+        e_sb = [keep.tile([P, S], F32, name=f"e_sb{t}", align_bytes=64) for t in range(PACK)]
+        top = keep.tile([P, 2, PACK], F32, name="top")
+        e_ps = {}
+
+        def second_stage(t, half):
+            e_ps[t, half] = psum.tile([P, HALF], F32, name=f"e_ps{t}{half}", tag=f"bank{PACK * half + t}")
+            for b in range(HP):
+                nc.tensor.matmul_mx(
+                    out=e_ps[t, half][:],
+                    lhsT=w4_w[:, b, t, :].bitcast(FP4X4), lhsT_scale=w4_s[:, b, t, :],
+                    rhs=h_w[b, half][:].bitcast(FP8X4), rhs_scale=h_s[b, half][:],
+                    start=(b == 0), stop=(b == HP - 1))
+
+        def drain_e(t, half):
+            nc.vector.tensor_scalar(
+                out=e_sb[t][:, half * HALF:(half + 1) * HALF], in0=e_ps[t, half][:],
+                scalar1=1.0, scalar2=None, op0=ALU.mult, op1=ALU.max,
+                accum_out=top[:, half, t:t + 1])
+
+        gather_words(0, 0, S)
+        nc.vector.tensor_copy(out=v_s[:], in_=tab_s[:].indirect(offs_sb[:]))
+        round_w1(0, 0, [("scalar", 0, P)])
+        quantize_w1(0, 0)
+        for c in range(NCH):
+            first_pass(0, 0, c)
+        gather_words(1, 0, S)
+        nc.vector.tensor_copy(out=w4_s[:].rearrange("p b t m -> p b m t"),
+                              in_=w4_sraw[:].rearrange("p b (m t) -> p b m t", t=PACK))
+        round_w1(0, 1, [("scalar", 0, P)])
+        round_w1(0, 2, [("vector", 0, P)])
+        quantize_w1(0, 1)
+        quantize_w1(0, 2)
+        for c in range(NCH):
+            first_pass(0, 1, c)
+        for d in range(NCH // 2):
+            gather_words(2, d * 2 * CH, (d + 1) * 2 * CH)
+            for c in (2 * d, 2 * d + 1):
+                first_pass(0, 2, c)
+                tanh_chunk(0, c)
+        round_w1(1, 0, [("vector", 0, P)])
+        round_w1(1, 1, [("scalar", 0, P)])
+        round_w1(1, 2, [("scalar", 0, P)])
+        gain_pair(0, 0)
+        quantize_w1(1, 0)
+        for c in range(NCH):
+            first_pass(1, 0, c)
+        gain_pair(0, 1)
+        quantize_h(0, 0)
+        gain_pair(0, 2)
+        quantize_h(0, 1)
+        quantize_w1(1, 1)
+        for c in range(NCH):
+            first_pass(1, 1, c)
+        gain_pair(0, 3)
+        quantize_h(0, 2)
+        quantize_w1(1, 2)
+        for c in range(NCH):
+            first_pass(1, 2, c)
+            tanh_chunk(1, c)
+        quantize_h(0, 3)
+        slope = keep.tile([P, PACK], F32, name="slope")
+        nc.vector.scalar_tensor_tensor(out=slope[:], in0=steep_sb[:], scalar=-1.0, in1=share_sb[:],
+                                       op0=ALU.mult, op1=ALU.mult)
+        gain_pair(1, 0)
+        gain_pair(1, 1)
+        quantize_h(1, 0)
+        gain_pair(1, 2)
+        quantize_h(1, 1)
+        for t in range(PACK):
+            second_stage(t, 0)
+        gain_pair(1, 3)
+        quantize_h(1, 2)
+        drain_e(0, 0)
+        quantize_h(1, 3)
+        for t in range(PACK):
+            second_stage(t, 1)
+        for t in range(1, PACK):
+            drain_e(t, 0)
+
+        bias = keep.tile([P, PACK], F32, name="bias")
+        y = keep.tile([P, PACK, M], F32, name="y", align_bytes=64)
+        out_rows = out_0.rearrange("(p t) m -> p t m", t=PACK)
+        gate = {}
+        plain = {}
+        best = {}
+
+        y_bf = keep.tile([P, M, PACK], BF16, name="y_bf", align_bytes=64)
+        y_w = keep.tile([P, M], U32, name="y_w", align_bytes=64)
+        y_s = keep.tile([P, M], U8, name="y_s", align_bytes=64)
+
+        def open_rows(t):
+            drain_e(t, 1)
+            nc.vector.tensor_scalar(out=bias[:, t:t + 1], in0=top[:, 0, t:t + 1], scalar1=top[:, 1, t:t + 1],
+                                    scalar2=slope[:, t:t + 1], op0=ALU.max, op1=ALU.mult)
+            gate[t] = ring.tile([P, M], F32, name="gate", bufs=2)
+            plain[t] = ring.tile([P, M], F32, name="plain", bufs=2)
+            best[t] = ring.tile([P, M], F32, name="best", bufs=2)
+
+        def look(t, m0, m1):
+            nc.scalar.activation(out=gate[t][:, m0:m1], in_=e_sb[t][:].indirect(pos1_sb[:, m0 // 16:m1 // 16]),
+                                 func=ACT.Sigmoid, bias=bias[:, t:t + 1], scale=steep_sb[:, t:t + 1])
+
+        def pick(t, m0, m1):
+            nc.vector.tensor_copy(out=plain[t][:, m0:m1],
+                                  in_=e_sb[t][:].indirect(pos2_sb[:, m0 // 16:m1 // 16]))
+
+        def join(t, m0, m1):
+            nc.vector.scalar_tensor_tensor(out=best[t][:, m0:m1], in0=gate[t][:, m0:m1],
+                                           scalar=worth_sb[:, t:t + 1], in1=plain[t][:, m0:m1],
+                                           op0=ALU.mult, op1=ALU.max)
+
+        def finish(t, m0, m1, engine):
+            if engine == "scalar":
+                nc.scalar.activation(out=y[:, t, m0:m1], in_=best[t][:, m0:m1], func=ACT.Copy,
+                                     scale=level_sb[:, t:t + 1])
+            else:
+                nc.vector.tensor_scalar(out=y[:, t, m0:m1], in0=best[t][:, m0:m1], scalar1=level_sb[:, t:t + 1],
+                                        scalar2=None, op0=ALU.mult)
+            nc.sync.dma_start(out_rows[:, t, m0:m1], y[:, t, m0:m1])
+
+        def round_y(m0, m1, engine):
+            dst = y_bf[:, m0:m1, :].rearrange("p (g i) t -> p g t i", i=4)
+            src = y[:, :, m0:m1].rearrange("p t (g i) -> p g t i", i=4)
+            if engine == "scalar":
+                nc.scalar.activation(out=dst, in_=src, func=ACT.Copy)
+            else:
+                nc.vector.tensor_copy(out=dst, in_=src)
+
+        last = PACK - 1
+        for t in range(last):
+            open_rows(t)
+            look(t, 0, M)
+            pick(t, 0, M)
+            if t > 0:
+                join(t - 1, 0, M)
+                finish(t - 1, 0, M, "scalar")
+        open_rows(last)
+        join(last - 1, 0, M)
+        look(last, 0, M // 2)
+        finish(last - 1, 0, M, "scalar")
+        look(last, M // 2, M)
+        for m0, m1 in ((0, M // 2), (M // 2, M)):
+            pick(last, m0, m1)
+            join(last, m0, m1)
+        finish(last, 0, M // 2, "scalar")
+        finish(last, M // 2, M, "vector")
+        round_y(0, M // 2, "scalar")
+        round_y(M // 2, M, "vector")
+        nc.vector.quantize_mx(out=y_w[:].bitcast(FP8X4), scales=y_s[:],
+                              in_=y_bf[:].rearrange("p m t -> p (m t)"))
+        nc.sync.dma_start(out_1[0].rearrange("p m t -> p (m t)").bitcast(I32), y_w[:].bitcast(I32))
+        for q in range(4):
+            queue = nc.sync if q % 2 == 0 else nc.scalar
+            queue.dma_start(out_2[0, 4 * q:4 * q + 4, :].bitcast(I32), y_s[32 * q:32 * q + 4, :].bitcast(I32))

@@ -41,7 +41,7 @@ def tile_list_prefetch_zone_scores_kernel(
         pos2_sb = keep.tile([P, M // 16], U16, name="pos2_sb")
         tab_w = [keep.tile([P, T], U32, name=f"tab_w{a}", align_bytes=64) for a in range(KP)]
         tab_s = keep.tile([P, T], U8, name="tab_s", align_bytes=64)
-        w1_raw = {(b, a): keep.tile([P, PACK, PASS], F32, name=f"w1_raw{b}{a}", align_bytes=64)
+        w1_raw = {(b, a): keep.tile([P, PACK, PASS], F32, name=f"w1_raw{b}{a}", tag=f"w1_raw{b}{a}", align_bytes=64)
                   for b in range(HP) for a in range(KP)}
         w4_raw = keep.tile([P, HP, 2 * N], U8, name="w4_raw", align_bytes=64)
         w4_sraw = keep.tile([P, HP, N], U8, name="w4_sraw", align_bytes=64)
@@ -61,7 +61,6 @@ def tile_list_prefetch_zone_scores_kernel(
 
         nc.vector.memset(tab_s[:].bitcast(I32), 0)
         nc.vector.memset(w4_sraw[:].bitcast(I32), 0)
-        nc.scalar.dma_start(gain_sb[:], gain.rearrange("(b p t) -> p b t", b=HP, t=PACK))
         nc.sync.dma_start(offs_sb[:], offs)
         nc.sync.dma_start(w4_raw[:].bitcast(I32), w4_words.rearrange("b p c -> p b c").bitcast(I32))
         load_tab(0)
@@ -71,6 +70,7 @@ def tile_list_prefetch_zone_scores_kernel(
                               tab_scales[:, 4 * q:4 * q + 4, :].bitcast(I32))
         load_tab(1)
         load_w1(0, 1)
+        nc.sync.dma_start(gain_sb[:], gain.rearrange("(b p t) -> p b t", b=HP, t=PACK))
         for q in range(4):
             nc.sync.dma_start(
                 w4_sraw[32 * q:32 * q + 4, :, :].bitcast(I32),
@@ -86,8 +86,8 @@ def tile_list_prefetch_zone_scores_kernel(
 
         w4_w = keep.tile([P, HP, PACK, 2 * P], U8, name="w4_w", align_bytes=64)
         w4_s = keep.tile([P, HP, PACK, P], U8, name="w4_s", align_bytes=64)
-        nc.vector.tensor_copy(out=w4_w[:].rearrange("p b t (m e) -> p b m t e", e=2),
-                              in_=w4_raw[:].rearrange("p b (m t e) -> p b m t e", t=PACK, e=2))
+        nc.vector.tensor_copy(out=w4_w[:].bitcast(U16).rearrange("p b t (g i) -> p b g t i", i=8),
+                              in_=w4_raw[:].bitcast(U16).rearrange("p b (g i t) -> p b g t i", t=PACK, i=8))
 
         v_w = [keep.tile([P, S], U32, name=f"v_w{a}", align_bytes=64) for a in range(KP)]
         v_s = keep.tile([P, S], U8, name="v_s", align_bytes=64)
@@ -100,15 +100,15 @@ def tile_list_prefetch_zone_scores_kernel(
         w1_w = {}
         w1_s = {}
 
-        def round_w1(b, a, shares):
-            w1_bf[b, a] = ring.tile([P, PACK, P, PACK], BF16, name="w1_bf", bufs=3, align_bytes=64)
-            dst = w1_bf[b, a][:].rearrange("p t m j -> p m j t")
-            src = w1_raw[b, a][:].rearrange("p j (m t) -> p m j t", t=PACK)
-            for engine, m0, m1 in shares:
-                if engine == "scalar":
-                    nc.scalar.activation(out=dst[:, m0:m1], in_=src[:, m0:m1], func=ACT.Copy)
-                else:
-                    nc.vector.tensor_copy(out=dst[:, m0:m1], in_=src[:, m0:m1])
+        def round_w1(b, a, m_vector):
+            w1_bf[b, a] = keep.tile([P, PACK, P, PACK], BF16, name=f"w1_bf{b}{a}", tag=f"w1_bf{b}{a}", align_bytes=64)
+            if m_vector > 0:
+                nc.vector.tensor_copy(out=w1_bf[b, a][:].rearrange("p t m j -> p m t j")[:, :m_vector],
+                                      in_=w1_raw[b, a][:].rearrange("p j (m t) -> p m t j", t=PACK)[:, :m_vector])
+            if m_vector < P:
+                nc.scalar.activation(out=w1_bf[b, a][:].rearrange("p t m j -> p m j t")[:, m_vector:],
+                                     in_=w1_raw[b, a][:].rearrange("p j (m t) -> p m j t", t=PACK)[:, m_vector:],
+                                     func=ACT.Copy)
 
         def quantize_w1(b, a):
             w1_w[b, a] = keep.tile([P, PASS], U32, name=f"w1_w{b}{a}", align_bytes=64)
@@ -135,17 +135,49 @@ def tile_list_prefetch_zone_scores_kernel(
         h_w = {}
         h_s = {}
 
+        gain_on_scalar = {(0, 3), (1, 2), (1, 3)}
+        h_pairs = {}
+
         def tanh_chunk(b, c):
+            d = c // 2
             if c % 2 == 0:
-                tanh_sb[b, c // 2] = ring.tile([P, 2, CH, PACK], F32, name="tanh_sb", align_bytes=64)
-            nc.scalar.activation(out=tanh_sb[b, c // 2][:, c % 2],
-                                 in_=acc[b, c][:].rearrange("p t n -> p n t"), func=ACT.Tanh)
+                tanh_sb[b, d] = ring.tile([P, 2 * CH * PACK], F32, name="tanh_sb", bufs=5, align_bytes=64)
+            if (b, d) in gain_on_scalar:
+                dst = tanh_sb[b, d][:].rearrange("p (t c n) -> p t c n", t=PACK, c=2)[:, :, c % 2, :]
+                nc.scalar.activation(out=dst, in_=acc[b, c][:], func=ACT.Tanh)
+            else:
+                dst = tanh_sb[b, d][:].rearrange("p (c n t) -> p c n t", t=PACK, c=2)[:, c % 2]
+                nc.scalar.activation(out=dst, in_=acc[b, c][:].rearrange("p t n -> p n t"), func=ACT.Tanh)
+
+        def new_h_bf(b, d):
+            if b == 0 and d % 2 == 0:
+                both = keep.tile([P, 2, 2 * CH, PACK], BF16, name=f"h_bf0{d}", tag=f"w1_bf1{1 + d // 2}",
+                                 align_bytes=64)
+                h_bf[0, d] = both[:, 0]
+                h_bf[0, d + 1] = both[:, 1]
+            elif b == 1:
+                h_bf[b, d] = ring.tile([P, 2 * CH, PACK], BF16, name="h_bf", align_bytes=64)
 
         def gain_pair(b, d):
-            h_bf[b, d] = ring.tile([P, 2 * CH, PACK], BF16, name="h_bf", align_bytes=64)
+            new_h_bf(b, d)
             nc.vector.tensor_tensor(
-                out=h_bf[b, d][:], in0=tanh_sb[b, d][:].rearrange("p c n t -> p (c n) t"),
+                out=h_bf[b, d][:], in0=tanh_sb[b, d][:].rearrange("p (n t) -> p n t", t=PACK),
                 in1=gain_sb[:, b:b + 1, :].to_broadcast([P, 2 * CH, PACK]), op=ALU.mult)
+
+        def gain_planes(b, d):
+            if b == 0:
+                h_pairs[b, d] = keep.tile([P, 2, 2 * CH, 2], BF16, name="h_pairs0", tag="w1_raw12", align_bytes=64)
+            else:
+                h_pairs[b, d] = ring.tile([P, 2, 2 * CH, 2], BF16, name="h_pairs", bufs=2, align_bytes=64)
+            src = tanh_sb[b, d][:].rearrange("p (t n) -> p t n", t=PACK)
+            for t in range(PACK):
+                nc.scalar.activation(out=h_pairs[b, d][:, t // 2, :, t % 2], in_=src[:, t, :], func=ACT.Copy,
+                                     scale=gain_sb[:, b, t:t + 1])
+
+        def weave_pairs(b, d):
+            new_h_bf(b, d)
+            nc.vector.tensor_copy(out=h_bf[b, d][:].bitcast(F32),
+                                  in_=h_pairs[b, d][:].bitcast(F32).rearrange("p u n e -> p n (u e)"))
 
         def quantize_h(b, d):
             half = d // 2
@@ -160,14 +192,14 @@ def tile_list_prefetch_zone_scores_kernel(
         top = keep.tile([P, 2, PACK], F32, name="top")
         e_ps = {}
 
-        def second_stage(t, half):
-            e_ps[t, half] = psum.tile([P, HALF], F32, name=f"e_ps{t}{half}", tag=f"bank{PACK * half + t}")
-            for b in range(HP):
-                nc.tensor.matmul_mx(
-                    out=e_ps[t, half][:],
-                    lhsT=w4_w[:, b, t, :].bitcast(FP4X4), lhsT_scale=w4_s[:, b, t, :],
-                    rhs=h_w[b, half][:].bitcast(FP8X4), rhs_scale=h_s[b, half][:],
-                    start=(b == 0), stop=(b == HP - 1))
+        def second_pass(t, half, b, j0, j1):
+            if b == 0:
+                e_ps[t, half] = psum.tile([P, HALF], F32, name=f"e_ps{t}{half}", tag=f"bank{PACK * half + t}")
+            nc.tensor.matmul_mx(
+                out=e_ps[t, half][:, j0:j1],
+                lhsT=w4_w[:, b, t, :].bitcast(FP4X4), lhsT_scale=w4_s[:, b, t, :],
+                rhs=h_w[b, half][:, j0:j1].bitcast(FP8X4), rhs_scale=h_s[b, half][:, j0:j1],
+                start=(b == 0), stop=(b == HP - 1 and j1 == HALF))
 
         def drain_e(t, half):
             nc.vector.tensor_scalar(
@@ -177,62 +209,67 @@ def tile_list_prefetch_zone_scores_kernel(
 
         gather_words(0, 0, S)
         nc.vector.tensor_copy(out=v_s[:], in_=tab_s[:].indirect(offs_sb[:]))
-        round_w1(0, 0, [("scalar", 0, P)])
+        round_w1(0, 0, 0)
         quantize_w1(0, 0)
         for c in range(NCH):
             first_pass(0, 0, c)
         gather_words(1, 0, S)
-        nc.vector.tensor_copy(out=w4_s[:].rearrange("p b t m -> p b m t"),
-                              in_=w4_sraw[:].rearrange("p b (m t) -> p b m t", t=PACK))
-        round_w1(0, 1, [("scalar", 0, P)])
-        round_w1(0, 2, [("vector", 0, P)])
+        nc.vector.tensor_copy(out=w4_s[:].rearrange("p b t (g i) -> p b g t i", i=16),
+                              in_=w4_sraw[:].rearrange("p b (g i t) -> p b g t i", t=PACK, i=16))
+        round_w1(0, 1, 0)
+        round_w1(0, 2, 80)
         quantize_w1(0, 1)
         quantize_w1(0, 2)
-        for c in range(NCH):
-            first_pass(0, 1, c)
         for d in range(NCH // 2):
             gather_words(2, d * 2 * CH, (d + 1) * 2 * CH)
             for c in (2 * d, 2 * d + 1):
+                first_pass(0, 1, c)
                 first_pass(0, 2, c)
                 tanh_chunk(0, c)
-        round_w1(1, 0, [("vector", 0, P)])
-        round_w1(1, 1, [("scalar", 0, P)])
-        round_w1(1, 2, [("scalar", 0, P)])
-        gain_pair(0, 0)
-        quantize_w1(1, 0)
+        round_w1(1, 2, 0)
+        for a in range(KP):
+            if a < KP - 1:
+                round_w1(1, a, P)
+            quantize_w1(1, a)
         for c in range(NCH):
-            first_pass(1, 0, c)
+            for a in range(KP):
+                first_pass(1, a, c)
+        gain_planes(0, 3)
+        gain_pair(0, 0)
         gain_pair(0, 1)
         quantize_h(0, 0)
         gain_pair(0, 2)
         quantize_h(0, 1)
-        quantize_w1(1, 1)
-        for c in range(NCH):
-            first_pass(1, 1, c)
-        gain_pair(0, 3)
+        weave_pairs(0, 3)
         quantize_h(0, 2)
-        quantize_w1(1, 2)
-        for c in range(NCH):
-            first_pass(1, 2, c)
-            tanh_chunk(1, c)
-        quantize_h(0, 3)
         slope = keep.tile([P, PACK], F32, name="slope")
-        nc.vector.scalar_tensor_tensor(out=slope[:], in0=steep_sb[:], scalar=-1.0, in1=share_sb[:],
-                                       op0=ALU.mult, op1=ALU.mult)
+        steep_share = keep.tile([P, PACK], F32, name="steep_share")
+        nc.gpsimd.tensor_tensor(out=steep_share[:], in0=steep_sb[:], in1=share_sb[:], op=ALU.mult)
+        nc.gpsimd.tensor_scalar(out=slope[:], in0=steep_share[:], scalar1=-1.0, scalar2=0.0,
+                                op0=ALU.mult, op1=ALU.add)
+        quantize_h(0, 3)
+        for c in range(6):
+            tanh_chunk(1, c)
+        gain_planes(1, 2)
+        for c in range(6, NCH):
+            tanh_chunk(1, c)
+        gain_planes(1, 3)
+        for t in range(PACK):
+            second_pass(t, 0, 0, 0, HALF)
         gain_pair(1, 0)
         gain_pair(1, 1)
         quantize_h(1, 0)
-        gain_pair(1, 2)
         quantize_h(1, 1)
         for t in range(PACK):
-            second_stage(t, 0)
-        gain_pair(1, 3)
-        quantize_h(1, 2)
-        drain_e(0, 0)
-        quantize_h(1, 3)
+            second_pass(t, 0, 1, 0, HALF)
         for t in range(PACK):
-            second_stage(t, 1)
-        for t in range(1, PACK):
+            second_pass(t, 1, 0, 0, HALF)
+        for d in (2, 3):
+            weave_pairs(1, d)
+            quantize_h(1, d)
+            for t in range(PACK):
+                second_pass(t, 1, 1, (d - 2) * 2 * CH, (d - 1) * 2 * CH)
+        for t in range(PACK):
             drain_e(t, 0)
 
         bias = keep.tile([P, PACK], F32, name="bias")

from contextlib import ExitStack

import concourse.mybir as mybir

K, T, S, M, H, N = 1536, 2048, 1024, 512, 1024, 512
FLOPS = 2 * K * H * S + 2 * H * N * S

F32 = mybir.dt.float32
BF16 = mybir.dt.bfloat16
I32 = mybir.dt.int32
U32 = mybir.dt.uint32
U16 = mybir.dt.uint16
U8 = mybir.dt.uint8
FP8X4 = mybir.dt.float8_e4m3fn_x4
FP4X4 = mybir.dt.float4_e2m1fn_x4
ALU = mybir.AluOpType
ACT = mybir.ActivationFunctionType

P = 128
PACK = 4
PASS = P * PACK
KP = K // PASS
HP = H // PASS
CH = 128
NCH = S // CH
HALF = 512


def tile_list_prefetch_zone_scores_kernel(
    tc, tab_words, tab_scales, w1, gain, w4_words, w4_scales, steep, share, worth, level,
    offs, pos1, pos2, out_0, out_1, out_2,
):
    nc = tc.nc
    with ExitStack() as ctx:
        keep = ctx.enter_context(tc.tile_pool(name="keep", bufs=1))
        ring = ctx.enter_context(tc.tile_pool(name="ring", bufs=4))
        psum = ctx.enter_context(tc.psum_pool(name="psum", bufs=1))

        offs_sb = keep.tile([P, S // 16], U16, name="offs_sb")
        pos1_sb = keep.tile([P, M // 16], U16, name="pos1_sb")
        pos2_sb = keep.tile([P, M // 16], U16, name="pos2_sb")
        tab_w = [keep.tile([P, T], U32, name=f"tab_w{a}", align_bytes=64) for a in range(KP)]
        tab_s = keep.tile([P, T], U8, name="tab_s", align_bytes=64)
        w1_raw = {(b, a): keep.tile([P, PACK, PASS], F32, name=f"w1_raw{b}{a}", tag=f"w1_raw{b}{a}", align_bytes=64)
                  for b in range(HP) for a in range(KP)}
        w4_raw = keep.tile([P, HP, 2 * N], U8, name="w4_raw", align_bytes=64)
        w4_sraw = keep.tile([P, HP, N], U8, name="w4_sraw", align_bytes=64)
        gain_sb = keep.tile([P, HP, PACK], F32, name="gain_sb")
        steep_sb = keep.tile([P, PACK], F32, name="steep_sb")
        share_sb = keep.tile([P, PACK], F32, name="share_sb")
        worth_sb = keep.tile([P, PACK], F32, name="worth_sb")
        level_sb = keep.tile([P, PACK], F32, name="level_sb")

        def load_tab(a):
            nc.sync.dma_start(tab_w[a][:].bitcast(I32),
                              tab_words[a].rearrange("p t i -> p (t i)").bitcast(I32))

        def load_w1(b, a):
            rows = w1[a * PASS:(a + 1) * PASS, b * PASS:(b + 1) * PASS]
            nc.sync.dma_start(w1_raw[b, a][:], rows.rearrange("(p j) c -> p j c", j=PACK))

        nc.vector.memset(tab_s[:].bitcast(I32), 0)
        nc.vector.memset(w4_sraw[:].bitcast(I32), 0)
        nc.sync.dma_start(offs_sb[:], offs)
        nc.sync.dma_start(w4_raw[:].bitcast(I32), w4_words.rearrange("b p c -> p b c").bitcast(I32))
        load_tab(0)
        load_w1(0, 0)
        for q in range(4):
            nc.sync.dma_start(tab_s[32 * q:32 * q + 4 * KP, :].bitcast(I32),
                              tab_scales[:, 4 * q:4 * q + 4, :].bitcast(I32))
        load_tab(1)
        load_w1(0, 1)
        nc.sync.dma_start(gain_sb[:], gain.rearrange("(b p t) -> p b t", b=HP, t=PACK))
        for q in range(4):
            nc.sync.dma_start(
                w4_sraw[32 * q:32 * q + 4, :, :].bitcast(I32),
                w4_scales[:, 4 * q:4 * q + 4, :].rearrange("b r c -> r b c").bitcast(I32))
        load_w1(0, 2)
        load_tab(2)
        for a in range(KP):
            load_w1(1, a)
        for vec_sb, vec in ((steep_sb, steep), (share_sb, share), (worth_sb, worth), (level_sb, level)):
            nc.sync.dma_start(vec_sb[:], vec.rearrange("(p t) -> p t", t=PACK))
        nc.sync.dma_start(pos1_sb[:], pos1)
        nc.sync.dma_start(pos2_sb[:], pos2)

        w4_w = keep.tile([P, HP, PACK, 2 * P], U8, name="w4_w", align_bytes=64)
        w4_s = keep.tile([P, HP, PACK, P], U8, name="w4_s", align_bytes=64)
        nc.vector.tensor_copy(out=w4_w[:].bitcast(U16).rearrange("p b t (g i) -> p b g t i", i=8),
                              in_=w4_raw[:].bitcast(U16).rearrange("p b (g i t) -> p b g t i", t=PACK, i=8))

        v_w = [keep.tile([P, S], U32, name=f"v_w{a}", align_bytes=64) for a in range(KP)]
        v_s = keep.tile([P, S], U8, name="v_s", align_bytes=64)

        def gather_words(a, j0, j1):
            nc.vector.tensor_copy(out=v_w[a][:, j0:j1],
                                  in_=tab_w[a][:].indirect(offs_sb[:, j0 // 16:j1 // 16]))

        w1_bf = {}
        w1_w = {}
        w1_s = {}

        def round_w1(b, a, m_vector):
            w1_bf[b, a] = keep.tile([P, PACK, P, PACK], BF16, name=f"w1_bf{b}{a}", tag=f"w1_bf{b}{a}", align_bytes=64)
            if m_vector > 0:
                nc.vector.tensor_copy(out=w1_bf[b, a][:].rearrange("p t m j -> p m t j")[:, :m_vector],
                                      in_=w1_raw[b, a][:].rearrange("p j (m t) -> p m t j", t=PACK)[:, :m_vector])
            if m_vector < P:
                nc.scalar.activation(out=w1_bf[b, a][:].rearrange("p t m j -> p m j t")[:, m_vector:],
                                     in_=w1_raw[b, a][:].rearrange("p j (m t) -> p m j t", t=PACK)[:, m_vector:],
                                     func=ACT.Copy)

        def quantize_w1(b, a):
            w1_w[b, a] = keep.tile([P, PASS], U32, name=f"w1_w{b}{a}", align_bytes=64)
            w1_s[b, a] = keep.tile([P, PASS], U8, name=f"w1_s{b}{a}", align_bytes=64)
            nc.vector.quantize_mx(out=w1_w[b, a][:].bitcast(FP8X4), scales=w1_s[b, a][:],
                                  in_=w1_bf[b, a][:].rearrange("p t m j -> p (t m j)"))

        acc = {}

        def first_pass(b, a, c):
            if a == 0:
                acc[b, c] = psum.tile([P, PACK, CH], F32, name=f"acc{b}{c}", tag=f"bank{c}")
            cols = slice(c * CH, (c + 1) * CH)
            for t in range(PACK):
                rows = slice(t * P, (t + 1) * P)
                nc.tensor.matmul_mx(
                    out=acc[b, c][:, t, :],
                    lhsT=w1_w[b, a][:, rows].bitcast(FP8X4), lhsT_scale=w1_s[b, a][:, rows],
                    rhs=v_w[a][:, cols].bitcast(FP8X4), rhs_scale=v_s[4 * a:P, cols],
                    start=(a == 0 and t == 0), stop=(a == KP - 1 and t == PACK - 1))

        tanh_sb = {}
        h_bf = {}
        h_w = {}
        h_s = {}

        gain_on_scalar = {(0, 3), (1, 2), (1, 3)}
        h_pairs = {}

        def tanh_chunk(b, c):
            d = c // 2
            if c % 2 == 0:
                tanh_sb[b, d] = ring.tile([P, 2 * CH * PACK], F32, name="tanh_sb", bufs=5, align_bytes=64)
            if (b, d) in gain_on_scalar:
                dst = tanh_sb[b, d][:].rearrange("p (t c n) -> p t c n", t=PACK, c=2)[:, :, c % 2, :]
                nc.scalar.activation(out=dst, in_=acc[b, c][:], func=ACT.Tanh)
            else:
                dst = tanh_sb[b, d][:].rearrange("p (c n t) -> p c n t", t=PACK, c=2)[:, c % 2]
                nc.scalar.activation(out=dst, in_=acc[b, c][:].rearrange("p t n -> p n t"), func=ACT.Tanh)

        def new_h_bf(b, d):
            if b == 0 and d % 2 == 0:
                both = keep.tile([P, 2, 2 * CH, PACK], BF16, name=f"h_bf0{d}", tag=f"w1_bf1{1 + d // 2}",
                                 align_bytes=64)
                h_bf[0, d] = both[:, 0]
                h_bf[0, d + 1] = both[:, 1]
            elif b == 1:
                h_bf[b, d] = ring.tile([P, 2 * CH, PACK], BF16, name="h_bf", align_bytes=64)

        def gain_pair(b, d):
            new_h_bf(b, d)
            nc.vector.tensor_tensor(
                out=h_bf[b, d][:], in0=tanh_sb[b, d][:].rearrange("p (n t) -> p n t", t=PACK),
                in1=gain_sb[:, b:b + 1, :].to_broadcast([P, 2 * CH, PACK]), op=ALU.mult)

        def gain_planes(b, d):
            if b == 0:
                h_pairs[b, d] = keep.tile([P, 2, 2 * CH, 2], BF16, name="h_pairs0", tag="w1_raw12", align_bytes=64)
            else:
                h_pairs[b, d] = ring.tile([P, 2, 2 * CH, 2], BF16, name="h_pairs", bufs=2, align_bytes=64)
            src = tanh_sb[b, d][:].rearrange("p (t n) -> p t n", t=PACK)
            for t in range(PACK):
                nc.scalar.activation(out=h_pairs[b, d][:, t // 2, :, t % 2], in_=src[:, t, :], func=ACT.Copy,
                                     scale=gain_sb[:, b, t:t + 1])

        def weave_pairs(b, d):
            new_h_bf(b, d)
            nc.vector.tensor_copy(out=h_bf[b, d][:].bitcast(F32),
                                  in_=h_pairs[b, d][:].bitcast(F32).rearrange("p u n e -> p n (u e)"))

        def quantize_h(b, d):
            half = d // 2
            if d % 2 == 0:
                h_w[b, half] = keep.tile([P, HALF], U32, name=f"h_w{b}{half}", align_bytes=64)
                h_s[b, half] = keep.tile([P, HALF], U8, name=f"h_s{b}{half}", align_bytes=64)
            cols = slice((d % 2) * 2 * CH, (d % 2 + 1) * 2 * CH)
            nc.vector.quantize_mx(out=h_w[b, half][:, cols].bitcast(FP8X4), scales=h_s[b, half][:, cols],
                                  in_=h_bf[b, d][:].rearrange("p n t -> p (n t)"))

        e_sb = [keep.tile([P, S], F32, name=f"e_sb{t}", align_bytes=64) for t in range(PACK)]
        top = keep.tile([P, 2, PACK], F32, name="top")
        e_ps = {}

        def second_pass(t, half, b, j0, j1):
            if b == 0:
                e_ps[t, half] = psum.tile([P, HALF], F32, name=f"e_ps{t}{half}", tag=f"bank{PACK * half + t}")
            nc.tensor.matmul_mx(
                out=e_ps[t, half][:, j0:j1],
                lhsT=w4_w[:, b, t, :].bitcast(FP4X4), lhsT_scale=w4_s[:, b, t, :],
                rhs=h_w[b, half][:, j0:j1].bitcast(FP8X4), rhs_scale=h_s[b, half][:, j0:j1],
                start=(b == 0), stop=(b == HP - 1 and j1 == HALF))

        def drain_e(t, half):
            nc.vector.tensor_scalar(
                out=e_sb[t][:, half * HALF:(half + 1) * HALF], in0=e_ps[t, half][:],
                scalar1=1.0, scalar2=None, op0=ALU.mult, op1=ALU.max,
                accum_out=top[:, half, t:t + 1])

        gather_words(0, 0, S)
        nc.vector.tensor_copy(out=v_s[:], in_=tab_s[:].indirect(offs_sb[:]))
        round_w1(0, 0, 0)
        quantize_w1(0, 0)
        for c in range(NCH):
            first_pass(0, 0, c)
        gather_words(1, 0, S)
        nc.vector.tensor_copy(out=w4_s[:].rearrange("p b t (g i) -> p b g t i", i=16),
                              in_=w4_sraw[:].rearrange("p b (g i t) -> p b g t i", t=PACK, i=16))
        round_w1(0, 1, 0)
        round_w1(0, 2, 80)
        quantize_w1(0, 1)
        quantize_w1(0, 2)
        for d in range(NCH // 2):
            gather_words(2, d * 2 * CH, (d + 1) * 2 * CH)
            for c in (2 * d, 2 * d + 1):
                first_pass(0, 1, c)
                first_pass(0, 2, c)
                tanh_chunk(0, c)
        round_w1(1, 2, 0)
        for a in range(KP):
            if a < KP - 1:
                round_w1(1, a, P)
            quantize_w1(1, a)
        for c in range(NCH):
            for a in range(KP):
                first_pass(1, a, c)
        gain_planes(0, 3)
        gain_pair(0, 0)
        gain_pair(0, 1)
        quantize_h(0, 0)
        gain_pair(0, 2)
        quantize_h(0, 1)
        weave_pairs(0, 3)
        quantize_h(0, 2)
        slope = keep.tile([P, PACK], F32, name="slope")
        steep_share = keep.tile([P, PACK], F32, name="steep_share")
        nc.gpsimd.tensor_tensor(out=steep_share[:], in0=steep_sb[:], in1=share_sb[:], op=ALU.mult)
        nc.gpsimd.tensor_scalar(out=slope[:], in0=steep_share[:], scalar1=-1.0, scalar2=0.0,
                                op0=ALU.mult, op1=ALU.add)
        quantize_h(0, 3)
        for c in range(6):
            tanh_chunk(1, c)
        gain_planes(1, 2)
        for c in range(6, NCH):
            tanh_chunk(1, c)
        gain_planes(1, 3)
        for t in range(PACK):
            second_pass(t, 0, 0, 0, HALF)
        gain_pair(1, 0)
        gain_pair(1, 1)
        quantize_h(1, 0)
        quantize_h(1, 1)
        for t in range(PACK):
            second_pass(t, 0, 1, 0, HALF)
        for t in range(PACK):
            second_pass(t, 1, 0, 0, HALF)
        for d in (2, 3):
            weave_pairs(1, d)
            quantize_h(1, d)
            for t in range(PACK):
                second_pass(t, 1, 1, (d - 2) * 2 * CH, (d - 1) * 2 * CH)
        for t in range(PACK):
            drain_e(t, 0)

        bias = keep.tile([P, PACK], F32, name="bias")
        y = keep.tile([P, PACK, M], F32, name="y", align_bytes=64)
        out_rows = out_0.rearrange("(p t) m -> p t m", t=PACK)
        gate = {}
        plain = {}
        best = {}

        y_bf = keep.tile([P, M, PACK], BF16, name="y_bf", align_bytes=64)
        y_w = keep.tile([P, M], U32, name="y_w", align_bytes=64)
        y_s = keep.tile([P, M], U8, name="y_s", align_bytes=64)

        def open_rows(t):
            drain_e(t, 1)
            nc.vector.tensor_scalar(out=bias[:, t:t + 1], in0=top[:, 0, t:t + 1], scalar1=top[:, 1, t:t + 1],
                                    scalar2=slope[:, t:t + 1], op0=ALU.max, op1=ALU.mult)
            gate[t] = ring.tile([P, M], F32, name="gate", bufs=2)
            plain[t] = ring.tile([P, M], F32, name="plain", bufs=2)
            best[t] = ring.tile([P, M], F32, name="best", bufs=2)

        def look(t, m0, m1):
            nc.scalar.activation(out=gate[t][:, m0:m1], in_=e_sb[t][:].indirect(pos1_sb[:, m0 // 16:m1 // 16]),
                                 func=ACT.Sigmoid, bias=bias[:, t:t + 1], scale=steep_sb[:, t:t + 1])

        def pick(t, m0, m1):
            nc.vector.tensor_copy(out=plain[t][:, m0:m1],
                                  in_=e_sb[t][:].indirect(pos2_sb[:, m0 // 16:m1 // 16]))

        def join(t, m0, m1):
            nc.vector.scalar_tensor_tensor(out=best[t][:, m0:m1], in0=gate[t][:, m0:m1],
                                           scalar=worth_sb[:, t:t + 1], in1=plain[t][:, m0:m1],
                                           op0=ALU.mult, op1=ALU.max)

        def finish(t, m0, m1, engine):
            if engine == "scalar":
                nc.scalar.activation(out=y[:, t, m0:m1], in_=best[t][:, m0:m1], func=ACT.Copy,
                                     scale=level_sb[:, t:t + 1])
            else:
                nc.vector.tensor_scalar(out=y[:, t, m0:m1], in0=best[t][:, m0:m1], scalar1=level_sb[:, t:t + 1],
                                        scalar2=None, op0=ALU.mult)
            nc.sync.dma_start(out_rows[:, t, m0:m1], y[:, t, m0:m1])

        def round_y(m0, m1, engine):
            dst = y_bf[:, m0:m1, :].rearrange("p (g i) t -> p g t i", i=4)
            src = y[:, :, m0:m1].rearrange("p t (g i) -> p g t i", i=4)
            if engine == "scalar":
                nc.scalar.activation(out=dst, in_=src, func=ACT.Copy)
            else:
                nc.vector.tensor_copy(out=dst, in_=src)

        last = PACK - 1
        for t in range(last):
            open_rows(t)
            look(t, 0, M)
            pick(t, 0, M)
            if t > 0:
                join(t - 1, 0, M)
                finish(t - 1, 0, M, "scalar")
        open_rows(last)
        join(last - 1, 0, M)
        look(last, 0, M // 2)
        finish(last - 1, 0, M, "scalar")
        look(last, M // 2, M)
        for m0, m1 in ((0, M // 2), (M // 2, M)):
            pick(last, m0, m1)
            join(last, m0, m1)
        finish(last, 0, M // 2, "scalar")
        finish(last, M // 2, M, "vector")
        round_y(0, M // 2, "scalar")
        round_y(M // 2, M, "vector")
        nc.vector.quantize_mx(out=y_w[:].bitcast(FP8X4), scales=y_s[:],
                              in_=y_bf[:].rearrange("p m t -> p (m t)"))
        nc.sync.dma_start(out_1[0].rearrange("p m t -> p (m t)").bitcast(I32), y_w[:].bitcast(I32))
        for q in range(4):
            queue = nc.sync if q % 2 == 0 else nc.scalar
            queue.dma_start(out_2[0, 4 * q:4 * q + 4, :].bitcast(I32), y_s[32 * q:32 * q + 4, :].bitcast(I32))
